import numpy as np, ml_dtypes
CORES = [2,3,42,43,82,83,122,123]
N = 8
import mx_ref
BF = ml_dtypes.bfloat16
def f(rng, *shape):
    return mx_ref.flush((rng.standard_normal(shape, dtype=np.float32) * np.exp2(rng.integers(-2, 3, shape[:-1] + (1,)))).astype(BF))
def wide(rng, *shape, cols=0):
    v = rng.standard_normal(shape, dtype=np.float32) * np.exp2(rng.integers(-12, 13, shape)).astype(np.float32)
    if cols: v *= np.repeat(np.exp2(rng.integers(-cols, cols + 1, shape[:-2] + (1, shape[-1] // 4))) * (rng.random(shape[:-2] + (1, shape[-1] // 4)) > 0.0625), 4, axis=-1).astype(np.float32)
    return mx_ref.flush(v.astype(BF))
PG, PW = 8, 128
def bare(d):
    d["sm"][:, :, 4 * PG:] = 0; d["gs"][:, :, 8:] = 0
    return d
def sizes(rng, d):
    for n in ("sm", "gs"): d[n] = mx_ref.flush((d[n].astype(np.float32) * np.exp2(rng.integers(-12, 13, (N, 1, 1))).astype(np.float32)).astype(BF))
    return d
def setup_inputs(rng):
    return bare({"pg": f(rng, N, 128 * PG, 4 * PW), "sm": f(rng, N, 128, 512), "gs": f(rng, N, 128, 512), "qw": f(rng, N, 128, 1024)})
def setup_inputs_ties(rng):
    d = setup_inputs(rng); v = d["sm"].reshape(N, 128, 128, 4).copy()
    for q in range(N):
        k = rng.integers(PG // 4 + 1, PG // 2 + 1); p = rng.permutation(PG)
        v[q][:, p[k:]] = v[q][:, p[np.arange(k, PG) % k]]
    d["sm"] = v.reshape(N, 128, 512)
    d = sizes(rng, d)
    for r in rng.permutation(N)[:2]: d["gs"][r][:, 4:8] = 0
    return d
def setup_inputs_last(rng):
    d = setup_inputs(rng); c = f(rng, 128, 4)
    for r in range(N):
        j = rng.integers(0, 2)
        d["gs"][r][:, 4 * j:4 * j + 4] = c
        d["sm"][r][:, 4 * PG - 4:4 * PG] = (c.astype(np.float32) * 2).astype(BF)
    return d
def setup_inputs_alike(rng):
    d = setup_inputs(rng); d["gs"] = np.stack([d["gs"][0]] * N); return d
def setup_inputs_below(rng):
    d = setup_inputs(rng)
    d["gs"] = np.abs(d["gs"].astype(np.float32)).astype(BF)
    d["sm"] = (-np.abs(d["sm"].astype(np.float32))).astype(BF)
    return bare(sizes(rng, d))
def setup_inputs_spread(rng):
    d = setup_inputs(rng); d["pg"] = wide(rng, N, 128 * PG, 4 * PW); d["sm"] = wide(rng, N, 128, 512); d["gs"] = wide(rng, N, 128, 512)
    return bare(d)
def check_inputs(d):
    b = []
    for r in range(N):
        if d["sm"][r][:, 4 * PG:].astype(np.float32).any(): b.append("sm")
        if d["gs"][r][:, 8:].astype(np.float32).any(): b.append("gs")
    return b
def reference(pg, sm, gs, qw):
    S = [mx_ref.quantize(t) for t in sm]; G = [mx_ref.quantize(t) for t in gs]
    y = np.zeros((N, 128, 2 * N * PW), np.float32); ch = np.zeros((N, 2, N), np.float32)
    for r in range(N):
        W = [mx_ref.quantize(qw[r][:, 512 * j:512 * j + 512]) for j in range(2)]
        for q in range(N):
            score = mx_ref.matmul(S[q], G[r])
            for j in range(2):
                c = int(np.argmax(score[:PG, j]))
                k = PW * (j * N + q)
                y[r][:, k:k + PW] = mx_ref.matmul(W[j], mx_ref.quantize(pg[q][128 * c:128 * c + 128]))
                ch[r, j, q] = c
    return {"y": y, "ch": ch}

@@ -1,0 +1,390 @@
+from concourse.bass import DstId, RemoteDMATransfer
+from concourse.mybir import dt, AluOpType, ActivationFunctionType
+
+U8 = dt.uint8
+N, PG, PW = 8, 8, 128
+NR = 6
+ROUNDS = [(1, 0, True), (3, 0, False), (1, 1, True), (3, 1, False), (2, 0, True), (2, 1, False)]
+NB1 = 3
+MATE, OWN = 6, 7
+NS = 640
+PLAN = [("choice", 0), ("choice", 1), ("serve", [0, 1, 2, MATE]), ("queries", 0), ("choice", 2), ("serve", [3, 4, 5, OWN]),
+        ("out", [OWN, MATE]), ("out", [1, 3]), ("out", [0, 2]), ("out", [5]), ("out", [4])]
+
+SCRATCH = {
+    "gsb": ("sbuf", [128, 512], "bfloat16"),
+    "smb": ("sbuf", [128, 512], "bfloat16"),
+    "qwb": ("sbuf", [128, 1024], "bfloat16"),
+    "pgb": ("sbuf", [128, 4096], "bfloat16"),
+    "tl": ("sbuf", [128, 8192], "bfloat16"),
+    "gt": ("sbuf", [128, 142], "float8_e4m3fn_x4"),
+    "gtp": ("sbuf", [128, 142], "uint8"),
+    "sc": ("sbuf", [128, 224], "float8_e4m3fn_x4"),
+    "scp": ("sbuf", [128, 224], "uint8"),
+    "wc": ("sbuf", [128, 256], "float8_e4m3fn_x4"),
+    "wp": ("sbuf", [128, 256], "uint8"),
+    "tc": ("sbuf", [128, 2048], "float8_e4m3fn_x4"),
+    "tp": ("sbuf", [128, 2048], "uint8"),
+    "rc": ("sbuf", [128, 2048], "float8_e4m3fn_x4"),
+    "rp": ("sbuf", [128, 2048], "uint8"),
+    "hc": ("sbuf", [128, 256 * NR], "float8_e4m3fn_x4"),
+    "hp": ("sbuf", [128, 256 * NR], "uint8"),
+    "hgc": ("sbuf", [128, 2], "float8_e4m3fn_x4"),
+    "hgp": ("sbuf", [128, 2], "uint8"),
+    "st": ("sbuf", [128, 96], "float32"),
+    "pm": ("sbuf", [128, 24], "float32"),
+    "lt": ("sbuf", [128, 192], "float32"),
+    "zz": ("sbuf", [128, 64], "float32"),
+    "ac": ("sbuf", [128, 192], "float32"),
+    "ct": ("sbuf", [128, 96], "float32"),
+    "cf": ("sbuf", [128, 96], "float32"),
+    "iop": ("sbuf", [128, 2], "int32"),
+    "ihi": ("sbuf", [128, 2], "int32"),
+    "fhi": ("sbuf", [128, 2], "float32"),
+    "io0": ("sbuf", [128, 32], "float32"),
+    "io1": ("sbuf", [128, 32], "float32"),
+    "off": ("sbuf", [128, 512], "uint16"),
+    "ysb": ("sbuf", [128, 2048], "float32"),
+    "chs": ("sbuf", [128, 8], "float32"),
+    "csrc": ("dram", [3, 128, 2], "float32"),
+    "cland": ("dram", [8, 128, 2], "float32"),
+    "ps": ("psum", [128, 4096], "float32"),
+}
+SEMAPHORES = (["ldg", "lds", "ldq", "ldp", "ms", "qg", "qs", "qw8", "cst", "ga1", "ga2", "cl", "sent", "hgc", "hgp", "std", "chf", "chd"]
+              + ["%s%d" % (n, b) for n in ("cps", "vc", "cfs", "cd") for b in range(3)]
+              + ["%s%d" % (n, d) for n in ("vo", "vg", "sg", "vq", "arr") for d in range(8)]
+              + ["%s%d" % (n, k) for n in ("hkc", "hkp") for k in range(NR)]
+              + ["%s%d" % (n, d) for n in ("pe", "ev") for d in range(16)])
+
+
+def bits(engines):
+    m = 0
+    for e in engines:
+        m |= 1 << e
+    return m
+
+
+def layout(T, topo):
+    cores = list(T.cores)
+    chips = []
+    for c in cores:
+        if topo.chip(c) not in chips:
+            chips.append(topo.chip(c))
+    rows = [[r for r in range(N) if topo.chip(cores[r]) == ch] for ch in chips]
+    place = {r: (x, y) for x in range(len(rows)) for y, r in enumerate(rows[x])}
+    nx = len(rows)
+
+    def asker(q, k):
+        x, y = place[q]
+        return rows[(x + ROUNDS[k][0]) % nx][y ^ ROUNDS[k][1]]
+
+    def owner(r, k):
+        x, y = place[r]
+        return rows[(x - ROUNDS[k][0]) % nx][y ^ ROUNDS[k][1]]
+
+    def mate(r):
+        x, y = place[r]
+        return rows[x][y ^ 1]
+
+    def helper(r):
+        c = cores[r]
+        far = [d for d in cores if topo.chip(d) != topo.chip(c)]
+        able = [h for h in topo.cores_of(c) if topo.die(h) != topo.die(c) and all(topo.may_write(h, d) for d in far)]
+        return able[place[r][1]]
+
+    return cores, asker, owner, mate, helper
+
+
+def dest(topo, core):
+    rid, pid, _ = topo.addr(core)
+    return DstId(rid=rid, pnc=pid)
+
+
+def write(g, topo, dst, out, in_, remote_sem, local_sem, engines):
+    rid, pid, _ = topo.addr(dst)
+    g.remote_dma(out, in_, remote_sem, local_sem, pid, rid, bits(engines))
+
+
+def gslot(k):
+    return k if k < NB1 else (NB1 if k == MATE else k + 1)
+
+
+def gcols(k):
+    return slice(128 + 2 * gslot(k), 130 + 2 * gslot(k))
+
+
+def fan(g, T, topo, core, cores, owners, out, in_, semname):
+    engines = topo.engines(core, cores[owners[0][0]])
+    g.remote_dma_fused([RemoteDMATransfer(
+        dst_ids=[dest(topo, cores[q]) for q, k in owners], dma_engine_mask=bits(engines), remote_sem=T.sem[semname],
+        srcs=[in_], dsts=[out(k) for q, k in owners], alu_op=0)], local_sem=T.sem.sent)
+    return len(engines)
+
+
+def stay(topo, core, near, far):
+    leave = topo.engines(core, far)
+    return [e for e in topo.engines(core, near) if e not in leave]
+
+
+def helper_program(g, core, T, topo, r, lay):
+    cores, asker, owner, mate, helper = lay
+    sent = 0
+    back = [(owner(r, k), k) for k in range(NB1, NR)]
+    half = len(stay(topo, cores[r], core, cores[back[0][0]])) // 2
+    g.wait_ge(T.sem.hgc, half)
+    sent += fan(g, T, topo, core, cores, back, lambda k: T.gt[:, gcols(k)].bitcast(U8), T.hgc[:, 0:2].bitcast(U8), "ga2")
+    g.wait_ge(T.sem.hgp, half)
+    sent += fan(g, T, topo, core, cores, back, lambda k: T.gtp[:, gcols(k)], T.hgp[:, 0:2], "ga2")
+    for k in range(NR):
+        if not ROUNDS[k][2]:
+            continue
+        a = cores[asker(r, k)]
+        off = topo.engines(core, a)
+        n = len(stay(topo, cores[r], core, a))
+        s, d = slice(256 * k, 256 * k + 256), slice(256 * r, 256 * r + 256)
+        g.wait_ge(T.sem["hkc%d" % k], n)
+        write(g, topo, a, T.rc[:, d].bitcast(U8), T.hc[:, s].bitcast(U8), T.sem["arr%d" % r], T.sem.sent, off)
+        g.wait_ge(T.sem["hkp%d" % k], n)
+        write(g, topo, a, T.rp[:, d], T.hp[:, s], T.sem["arr%d" % r], T.sem.sent, off)
+        sent += 2 * len(off)
+    g.wait_ge(T.sem.sent, sent)
+
+
+def rank_program(g, core, T, topo):
+    lay = layout(T, topo)
+    cores, asker, owner, mate, helper = lay
+    rank = T.rank_of(core)
+    if rank is None:
+        for r in range(N):
+            if helper(r) == core:
+                helper_program(g, core, T, topo, r, lay)
+        return
+    V, S, P, Y, sem = g.vector, g.scalar, g.tensor, g.sync, T.sem
+    A, COPY = AluOpType, ActivationFunctionType.Copy
+    m, h = mate(rank), helper(rank)
+    off = topo.engines(core, cores[asker(rank, 0)])
+    loc = stay(topo, core, cores[m], cores[asker(rank, 0)])
+    lh = len(loc) // 2
+    who = [asker(rank, k) for k in range(NR)] + [m, rank]
+    src = [owner(rank, k) for k in range(NR)] + [m, rank]
+    served = [d for kind, x in PLAN if kind == "serve" for d in x]
+    flow = [d for kind, x in PLAN if kind == "out" for d in x]
+    item = {d: i for i, d in enumerate(flow)}
+
+    Y.dma_start(T.gsb[:], T.gs[:]).then_inc(sem.ldg, 16)
+    S.dma_start(T.smb[:], T.sm[:]).then_inc(sem.lds, 16)
+    for p in range(0, PG, 2):
+        Y.dma_start(T.pgb[:, 512 * p:512 * p + 512], T.pg[128 * p:128 * p + 128, :]).then_inc(sem.ldp, 16)
+        S.dma_start(T.pgb[:, 512 * p + 512:512 * p + 1024], T.pg[128 * p + 128:128 * p + 256, :]).then_inc(sem.ldp, 16)
+    S.wait_ge(sem.vc0, 5)
+    S.dma_start(T.qwb[:], T.qw[:]).then_inc(sem.ldq, 16)
+
+    V.memset(T.lt[:], 0.0).then_inc(sem.ms, 1)
+    V.memset(T.zz[:], 0.0).then_inc(sem.ms, 1)
+    g.iota(T.iop[:], [[0, 2]], 0, 1).then_inc(sem.cst, 1)
+    g.iota(T.io0[:], [[16, 32]], 0, 1, allow_small_or_imprecise_dtypes=True).then_inc(sem.cst, 1)
+    V.wait_ge(sem.cst, 2)
+    V.tensor_scalar(T.ihi[:], T.iop[:], 112, None, A.bitwise_and).then_inc(sem.cst, 1)
+    V.wait_ge(sem.cst, 3)
+    V.tensor_copy(T.fhi[:], T.ihi[:]).then_inc(sem.cst, 1)
+    V.wait_ge(sem.cst, 4)
+    V.tensor_scalar(T.io1[:], T.io0[:], T.fhi[:, 0:1], None, A.subtract).then_inc(sem.cst, 1)
+    V.wait_ge(sem.cst, 5)
+    V.wait_ge(sem.ms, 2)
+    V.wait_ge(sem.ldg, 16)
+    V.quantize_mx(T.gt[:, 0:128], T.gtp[:, 0:128], T.gsb[:]).then_inc(sem.qg, 1)
+    V.wait_ge(sem.lds, 16)
+    for a in range(4):
+        if a:
+            V.wait_ge(sem.qs, a)
+        V.quantize_mx(T.sc[:, 32 * a:32 * a + 128], T.scp[:, 32 * a:32 * a + 128], T.smb[:]).then_inc(sem.qs, 1)
+
+    ends = [128, 128 + 2 * (NB1 + 1), 142]
+    low = [0, 96, 96]
+    head = [0, 32 - 2 * (NB1 + 1), 32 - 2 * (NR - NB1)]
+
+    def colof(d):
+        if d == OWN:
+            return 0, 0
+        if d == MATE or d < NB1:
+            return 1, head[1] + 2 * gslot(d)
+        return 2, head[2] + 2 * (d - NB1)
+
+    def choice(b):
+        c, e = 32 * b, 64 * b
+        vc = sem["vc%d" % b]
+        V.wait_ge(sem["cps%d" % b], 1)
+        V.transpose(T.st[:, c:c + 32], T.ps[:, low[b]:low[b] + 32]).then_inc(vc, 1)
+        V.wait_ge(vc, 1)
+        V.tensor_tensor_scan(T.pm[:, 8 * b:8 * b + 8], T.st[:, c:c + 8], T.st[:, c:c + 8], T.st[:, c:c + 1], A.max, A.max).then_inc(vc, 1)
+        V.wait_ge(vc, 2)
+        V.tensor_scalar(T.lt[:, e + 24:e + 32], T.pm[:, 8 * b:8 * b + 8], T.pm[:, 8 * b + 7:8 * b + 8], 512.0, A.is_lt, A.mult).then_inc(vc, 1)
+        V.wait_ge(vc, 3)
+        V.tensor_tensor_scan(T.ac[:, e + 24:e + 64], T.lt[:, e + 24:e + 64], T.zz[:, 24:64], 0.0, A.add, A.add).then_inc(vc, 1)
+        V.wait_ge(vc, 4)
+        V.transpose(T.ct[:, c:c + 32], T.ac[:, e + 32:e + 64]).then_inc(vc, 1)
+        V.wait_ge(vc, 5)
+
+    def numbers(b):
+        c = 32 * b
+        V.tensor_scalar(T.cf[:, c:c + 32], T.ct[:, c:c + 32], 1.0 / 512, None, A.mult).then_inc(sem["cfs%d" % b], 1)
+
+    def offsets(d):
+        b, c = colof(d)
+        for j in range(2):
+            k = 64 * d + 32 * j
+            V.tensor_scalar(T.off[:, k:k + 32], T.io1[:], T.ct[:, 32 * b + c + j:32 * b + c + j + 1], None, A.add).then_inc(sem["vo%d" % d], 1)
+
+    def serve(order, b):
+        offsets(order[0])
+        for i, d in enumerate(order):
+            if i == 0 and len(order) > 1:
+                offsets(order[1])
+            V.wait_ge(sem["vo%d" % d], 2)
+            V.tensor_copy(T.tl[:, 1024 * d + NS:1024 * d + 1024],
+                          T.pgb[:, 0:4096].indirect(T.off[:, 64 * d + NS // 16:64 * d + 64])).then_inc(sem["vg%d" % d], 1)
+            if i + 2 < len(order):
+                offsets(order[i + 2])
+            if i == min(1, len(order) - 1) and b:
+                numbers(b)
+            V.wait_ge(sem["vg%d" % d], 1)
+            V.wait_ge(sem["sg%d" % d], 1)
+            V.quantize_mx(T.tc[:, 256 * d:256 * d + 256], T.tp[:, 256 * d:256 * d + 256], T.tl[:, 1024 * d:1024 * d + 1024]).then_inc(sem["vq%d" % d], 1)
+
+    stores = [0]
+
+    def bank(n):
+        return 512 * (1 + n % 7)
+
+    def store(q, gr, j):
+        qs = sorted(src[d] for d in gr)
+        for d in gr:
+            q.wait_ge(sem["ev%d" % (2 * item[d] + j)], 1)
+        runs = [[qs[0]]]
+        for x in qs[1:]:
+            if x == runs[-1][-1] + 1:
+                runs[-1].append(x)
+            else:
+                runs.append([x])
+        for run in runs:
+            a, b = PW * (j * N + run[0]), PW * (j * N + run[-1] + 1)
+            q.dma_start(T.y[:, a:b], T.ysb[:, a:b]).then_inc(sem.std, 16)
+            stores[0] += 16
+
+    def product(d):
+        if d == OWN:
+            P.wait_ge(sem["vq%d" % OWN], 1)
+            buf, pl, c0 = T.tc, T.tp, 256 * OWN
+        else:
+            P.wait_ge(sem["arr%d" % src[d]], 2 * (len(loc) if d == MATE else len(off)))
+            buf, pl, c0 = T.rc, T.rp, 256 * src[d]
+        for j in range(2):
+            n = 2 * item[d] + j
+            if n >= 7:
+                P.wait_ge(sem["ev%d" % (n - 7)], 1)
+            c, w = slice(c0 + 128 * j, c0 + 128 * j + 128), slice(128 * j, 128 * j + 128)
+            P.matmul_mx(T.ps[:, bank(n):bank(n) + 128], T.wc[:, w], T.wp[:, w], buf[:, c], pl[:, c], True, True).then_inc(sem["pe%d" % n], 1)
+
+    arrived = [0, 2 * len(off) * NB1 + 2 * lh, 2 * len(off) * (NR - NB1)]
+    batch = [0]
+    paged = [False]
+    for kind, x in PLAN:
+        if kind == "choice":
+            if x:
+                P.wait_ge(sem["vc%d" % (x - 1)], 1)
+                P.wait_ge(sem["ga%d" % x], arrived[x])
+            else:
+                P.wait_ge(sem.qg, 1)
+                P.wait_ge(sem.qs, 4)
+            v = slice(ends[x] - 128, ends[x])
+            P.matmul_mx(T.ps[:, 0:128], T.sc[:, 0:128], T.scp[:, 0:128], T.gt[:, v], T.gtp[:, v], True, True).then_inc(sem["cps%d" % x], 1)
+            choice(x)
+            batch[0] = x
+            if x == 0:
+                numbers(0)
+        elif kind == "queries":
+            V.wait_ge(sem.ldq, 16)
+            V.quantize_mx(T.wc[:], T.wp[:], T.qwb[:]).then_inc(sem.qw8, 1)
+        elif kind == "serve":
+            if not paged[0]:
+                V.wait_ge(sem.ldp, 16 * PG)
+                S.wait_ge(sem.ldp, 16 * PG)
+                paged[0] = True
+            serve(x, batch[0])
+            for d in x:
+                S.wait_ge(sem["vo%d" % d], 2)
+                S.activation(T.tl[:, 1024 * d:1024 * d + NS], T.pgb[:, 0:4096].indirect(T.off[:, 64 * d:64 * d + NS // 16]), COPY).then_inc(sem["sg%d" % d], 1)
+        else:
+            if x[0] == flow[0]:
+                P.wait_ge(sem.qw8, 1)
+            for d in x:
+                product(d)
+                n, k = 2 * item[d], PW * src[d]
+                V.wait_ge(sem["pe%d" % n], 1)
+                V.tensor_copy(T.ysb[:, k:k + PW], T.ps[:, bank(n):bank(n) + 128]).then_inc(sem["ev%d" % n], 1)
+                n, k = n + 1, k + PW * N
+                S.wait_ge(sem["pe%d" % n], 1)
+                S.activation(T.ysb[:, k:k + PW], T.ps[:, bank(n):bank(n) + 128], COPY).then_inc(sem["ev%d" % n], 1)
+            store(S, x, 1)
+
+    sent = 0
+    front = [(owner(rank, k), k) for k in range(NB1)]
+    g.wait_ge(sem.qg, 1)
+    sent += fan(g, T, topo, core, cores, front, lambda k: T.gt[:, gcols(k)].bitcast(U8), T.gt[:, 0:2].bitcast(U8), "ga1")
+    sent += fan(g, T, topo, core, cores, front, lambda k: T.gtp[:, gcols(k)], T.gtp[:, 0:2], "ga1")
+
+    def near(outs, in_, sems):
+        g.remote_dma_fused([RemoteDMATransfer(dst_ids=[dest(topo, c)], dma_engine_mask=bits(loc[lh * i:lh * i + lh]), remote_sem=sems[i],
+                                              srcs=[in_], dsts=[outs[i]], alu_op=0) for i, c in enumerate((h, cores[m]))], local_sem=sem.sent)
+        return 2 * lh
+
+    sent += near([T.hgc[:, 0:2].bitcast(U8), T.gt[:, gcols(MATE)].bitcast(U8)], T.gt[:, 0:2].bitcast(U8), [sem.hgc, sem.ga1])
+    sent += near([T.hgp[:, 0:2], T.gtp[:, gcols(MATE)]], T.gtp[:, 0:2], [sem.hgp, sem.ga1])
+
+    def pages(d):
+        s, t = slice(256 * d, 256 * d + 256), slice(256 * rank, 256 * rank + 256)
+        g.wait_ge(sem["vq%d" % d], 1)
+        if d < NR and ROUNDS[d][2]:
+            write(g, topo, h, T.hc[:, s].bitcast(U8), T.tc[:, s].bitcast(U8), sem["hkc%d" % d], sem.sent, loc)
+            write(g, topo, h, T.hp[:, s], T.tp[:, s], sem["hkp%d" % d], sem.sent, loc)
+            return 2 * len(loc)
+        e, a = (loc if d == MATE else off), cores[who[d]]
+        write(g, topo, a, T.rc[:, t].bitcast(U8), T.tc[:, s].bitcast(U8), sem["arr%d" % rank], sem.sent, e)
+        write(g, topo, a, T.rp[:, t], T.tp[:, s], sem["arr%d" % rank], sem.sent, e)
+        return 2 * len(e)
+
+    def choices(b, slots):
+        g.wait_ge(sem["cd%d" % b], 16)
+        g.remote_dma_fused([RemoteDMATransfer(dst_ids=[dest(topo, cores[who[d]])], dma_engine_mask=bits([loc[0] if d == MATE else off[i]]),
+                                              remote_sem=sem.cl, srcs=[T.csrc[b]], dsts=[T.cland[rank]], alu_op=0)
+                            for i, d in enumerate(slots)], local_sem=sem.sent)
+        return len(slots)
+
+    told = [False]
+    for d in served:
+        if d == OWN:
+            continue
+        if colof(d)[0] == 2 and not told[0]:
+            sent += choices(1, list(range(NB1)) + [MATE])
+            told[0] = True
+        sent += pages(d)
+    sent += choices(2, list(range(NB1, NR)))
+
+    Y.wait_ge(sem.cfs0, 1)
+    Y.dma_start(T.chs[0:2, rank:rank + 1], T.cf[0:1, 0:2]).then_inc(sem.chf, 16)
+    for b in (1, 2):
+        Y.wait_ge(sem["cfs%d" % b], 1)
+        Y.dma_start(T.csrc[b], T.cf[0:8, 32 * b:32 * b + 32]).then_inc(sem["cd%d" % b], 16)
+    groups = [x for kind, x in PLAN if kind == "out"]
+    for i, gr in enumerate(groups):
+        if i == len(groups) - 2:
+            Y.wait_ge(sem.cl, N - 1)
+            for d in range(NR + 1):
+                q, c = src[d], colof(d)[1] // 2
+                Y.dma_start(T.chs[0:2, q:q + 1], T.cland[q, c:c + 1, 0:2]).then_inc(sem.chf, 16)
+        store(Y, gr, 0)
+    Y.wait_ge(sem.chf, 16 * N)
+    Y.dma_start(T.ch[:], T.chs[0:2, 0:8]).then_inc(sem.chd, 16)
+    Y.wait_ge(sem.chd, 16)
+    Y.wait_ge(sem.std, stores[0])
+    g.wait_ge(sem.sent, sent)

@@ -4,12 +4,14 @@ from concourse.mybir import dt, AluOpType, ActivationFunctionType
 U8 = dt.uint8
 N, PG, PW = 8, 8, 128
 NR = 6
-ROUNDS = [(1, 0, True), (3, 0, False), (1, 1, True), (3, 1, False), (2, 0, True), (2, 1, False)]
+ROUNDS = [(2, 0, True), (1, 0, False), (1, 1, True), (2, 1, False), (3, 0, True), (3, 1, False)]
 NB1 = 3
 MATE, OWN = 6, 7
 NS = 640
-PLAN = [("choice", 0), ("choice", 1), ("serve", [0, 1, 2, MATE]), ("queries", 0), ("choice", 2), ("serve", [3, 4, 5, OWN]),
-        ("out", [OWN, MATE]), ("out", [1, 3]), ("out", [0, 2]), ("out", [5]), ("out", [4])]
+VPLAN = "c0 c1 o0 o1 n1 g0 o2 q0 g1 o7 q1 g2 q2 c2 o3 o4 n2 g3 o5 q3 g4 o6 q4 g5 q5 w0 g6 q6 g7 q7 e0 e1 e2 e3 e4"
+GATHERS = [0, 1, 2, OWN, 3, 4, 5, MATE]
+OUTS = [[0, 3], [1, 2], [OWN, MATE], [5], [4]]
+LATE = 1
 
 SCRATCH = {
     "gsb": ("sbuf", [128, 512], "bfloat16"),
@@ -167,17 +169,18 @@ def rank_program(g, core, T, topo):
     lh = len(loc) // 2
     who = [asker(rank, k) for k in range(NR)] + [m, rank]
     src = [owner(rank, k) for k in range(NR)] + [m, rank]
-    served = [d for kind, x in PLAN if kind == "serve" for d in x]
-    flow = [d for kind, x in PLAN if kind == "out" for d in x]
+    steps = [(t[0], int(t[1])) for t in VPLAN.split()]
+    flow = [d for gr in OUTS for d in gr]
     item = {d: i for i, d in enumerate(flow)}
 
-    Y.dma_start(T.gsb[:], T.gs[:]).then_inc(sem.ldg, 16)
-    S.dma_start(T.smb[:], T.sm[:]).then_inc(sem.lds, 16)
-    for p in range(0, PG, 2):
-        Y.dma_start(T.pgb[:, 512 * p:512 * p + 512], T.pg[128 * p:128 * p + 128, :]).then_inc(sem.ldp, 16)
-        S.dma_start(T.pgb[:, 512 * p + 512:512 * p + 1024], T.pg[128 * p + 128:128 * p + 256, :]).then_inc(sem.ldp, 16)
-    S.wait_ge(sem.vc0, 5)
-    S.dma_start(T.qwb[:], T.qw[:]).then_inc(sem.ldq, 16)
+    Y.dma_start(T.gsb[:, 0:256], T.gs[:, 0:256]).then_inc(sem.ldg, 16)
+    S.dma_start(T.gsb[:, 256:512], T.gs[:, 256:512]).then_inc(sem.ldg, 16)
+    Y.dma_start(T.smb[:], T.sm[:]).then_inc(sem.lds, 16)
+    for p in range(PG):
+        q = S if p % 2 == 0 or p >= PG - LATE else Y
+        if p == PG - LATE:
+            S.wait_ge(sem.vc0, 5)
+        q.dma_start(T.pgb[:, 512 * p:512 * p + 512], T.pg[128 * p:128 * p + 128, :]).then_inc(sem.ldp, 16)
 
     V.memset(T.lt[:], 0.0).then_inc(sem.ms, 1)
     V.memset(T.zz[:], 0.0).then_inc(sem.ms, 1)
@@ -191,7 +194,7 @@ def rank_program(g, core, T, topo):
     V.tensor_scalar(T.io1[:], T.io0[:], T.fhi[:, 0:1], None, A.subtract).then_inc(sem.cst, 1)
     V.wait_ge(sem.cst, 5)
     V.wait_ge(sem.ms, 2)
-    V.wait_ge(sem.ldg, 16)
+    V.wait_ge(sem.ldg, 32)
     V.quantize_mx(T.gt[:, 0:128], T.gtp[:, 0:128], T.gsb[:]).then_inc(sem.qg, 1)
     V.wait_ge(sem.lds, 16)
     for a in range(4):
@@ -235,26 +238,70 @@ def rank_program(g, core, T, topo):
             k = 64 * d + 32 * j
             V.tensor_scalar(T.off[:, k:k + 32], T.io1[:], T.ct[:, 32 * b + c + j:32 * b + c + j + 1], None, A.add).then_inc(sem["vo%d" % d], 1)
 
-    def serve(order, b):
-        offsets(order[0])
-        for i, d in enumerate(order):
-            if i == 0 and len(order) > 1:
-                offsets(order[1])
-            V.wait_ge(sem["vo%d" % d], 2)
-            V.tensor_copy(T.tl[:, 1024 * d + NS:1024 * d + 1024],
-                          T.pgb[:, 0:4096].indirect(T.off[:, 64 * d + NS // 16:64 * d + 64])).then_inc(sem["vg%d" % d], 1)
-            if i + 2 < len(order):
-                offsets(order[i + 2])
-            if i == min(1, len(order) - 1) and b:
-                numbers(b)
-            V.wait_ge(sem["vg%d" % d], 1)
-            V.wait_ge(sem["sg%d" % d], 1)
-            V.quantize_mx(T.tc[:, 256 * d:256 * d + 256], T.tp[:, 256 * d:256 * d + 256], T.tl[:, 1024 * d:1024 * d + 1024]).then_inc(sem["vq%d" % d], 1)
+    arrived = [0, 2 * len(off) * NB1 + 2 * lh, 2 * len(off) * (NR - NB1)]
 
-    stores = [0]
+    def scores(b):
+        if b:
+            P.wait_ge(sem["vc%d" % (b - 1)], 1)
+            P.wait_ge(sem["ga%d" % b], arrived[b])
+        else:
+            P.wait_ge(sem.qg, 1)
+            P.wait_ge(sem.qs, 4)
+        v = slice(ends[b] - 128, ends[b])
+        P.matmul_mx(T.ps[:, 0:128], T.sc[:, 0:128], T.scp[:, 0:128], T.gt[:, v], T.gtp[:, v], True, True).then_inc(sem["cps%d" % b], 1)
 
     def bank(n):
         return 512 * (1 + n % 7)
+
+    def product(d):
+        if d == OWN:
+            P.wait_ge(sem["vq%d" % OWN], 1)
+            buf, pl, c0 = T.tc, T.tp, 256 * OWN
+        else:
+            P.wait_ge(sem["arr%d" % src[d]], 2 * (len(loc) if d == MATE else len(off)))
+            buf, pl, c0 = T.rc, T.rp, 256 * src[d]
+        for j in range(2):
+            n = 2 * item[d] + j
+            if n >= 7:
+                P.wait_ge(sem["ev%d" % (n - 7)], 1)
+            c, w = slice(c0 + 128 * j, c0 + 128 * j + 128), slice(128 * j, 128 * j + 128)
+            P.matmul_mx(T.ps[:, bank(n):bank(n) + 128], T.wc[:, w], T.wp[:, w], buf[:, c], pl[:, c], True, True).then_inc(sem["pe%d" % n], 1)
+
+    for b in range(3):
+        scores(b)
+    P.wait_ge(sem.qw8, 1)
+    for d in flow:
+        product(d)
+
+    for kind, x in steps:
+        if kind == "c":
+            choice(x)
+            if x == 0:
+                numbers(0)
+            if x == 1:
+                V.wait_ge(sem.ldp, 16 * PG)
+        elif kind == "w":
+            V.wait_ge(sem.ldq, 16)
+            V.quantize_mx(T.wc[:], T.wp[:], T.qwb[:]).then_inc(sem.qw8, 1)
+        elif kind == "o":
+            offsets(x)
+        elif kind == "n":
+            numbers(x)
+        elif kind == "g":
+            V.wait_ge(sem["vo%d" % x], 2)
+            V.tensor_copy(T.tl[:, 1024 * x + NS:1024 * x + 1024],
+                          T.pgb[:, 0:4096].indirect(T.off[:, 64 * x + NS // 16:64 * x + 64])).then_inc(sem["vg%d" % x], 1)
+        elif kind == "q":
+            V.wait_ge(sem["vg%d" % x], 1)
+            V.wait_ge(sem["sg%d" % x], 1)
+            V.quantize_mx(T.tc[:, 256 * x:256 * x + 256], T.tp[:, 256 * x:256 * x + 256], T.tl[:, 1024 * x:1024 * x + 1024]).then_inc(sem["vq%d" % x], 1)
+        else:
+            for d in OUTS[x]:
+                n, k = 2 * item[d], PW * src[d]
+                V.wait_ge(sem["pe%d" % n], 1)
+                V.tensor_copy(T.ysb[:, k:k + PW], T.ps[:, bank(n):bank(n) + 128]).then_inc(sem["ev%d" % n], 1)
+
+    stores = [0]
 
     def store(q, gr, j):
         qs = sorted(src[d] for d in gr)
@@ -271,61 +318,16 @@ def rank_program(g, core, T, topo):
             q.dma_start(T.y[:, a:b], T.ysb[:, a:b]).then_inc(sem.std, 16)
             stores[0] += 16
 
-    def product(d):
-        if d == OWN:
-            P.wait_ge(sem["vq%d" % OWN], 1)
-            buf, pl, c0 = T.tc, T.tp, 256 * OWN
-        else:
-            P.wait_ge(sem["arr%d" % src[d]], 2 * (len(loc) if d == MATE else len(off)))
-            buf, pl, c0 = T.rc, T.rp, 256 * src[d]
-        for j in range(2):
-            n = 2 * item[d] + j
-            if n >= 7:
-                P.wait_ge(sem["ev%d" % (n - 7)], 1)
-            c, w = slice(c0 + 128 * j, c0 + 128 * j + 128), slice(128 * j, 128 * j + 128)
-            P.matmul_mx(T.ps[:, bank(n):bank(n) + 128], T.wc[:, w], T.wp[:, w], buf[:, c], pl[:, c], True, True).then_inc(sem["pe%d" % n], 1)
-
-    arrived = [0, 2 * len(off) * NB1 + 2 * lh, 2 * len(off) * (NR - NB1)]
-    batch = [0]
-    paged = [False]
-    for kind, x in PLAN:
-        if kind == "choice":
-            if x:
-                P.wait_ge(sem["vc%d" % (x - 1)], 1)
-                P.wait_ge(sem["ga%d" % x], arrived[x])
-            else:
-                P.wait_ge(sem.qg, 1)
-                P.wait_ge(sem.qs, 4)
-            v = slice(ends[x] - 128, ends[x])
-            P.matmul_mx(T.ps[:, 0:128], T.sc[:, 0:128], T.scp[:, 0:128], T.gt[:, v], T.gtp[:, v], True, True).then_inc(sem["cps%d" % x], 1)
-            choice(x)
-            batch[0] = x
-            if x == 0:
-                numbers(0)
-        elif kind == "queries":
-            V.wait_ge(sem.ldq, 16)
-            V.quantize_mx(T.wc[:], T.wp[:], T.qwb[:]).then_inc(sem.qw8, 1)
-        elif kind == "serve":
-            if not paged[0]:
-                V.wait_ge(sem.ldp, 16 * PG)
-                S.wait_ge(sem.ldp, 16 * PG)
-                paged[0] = True
-            serve(x, batch[0])
-            for d in x:
-                S.wait_ge(sem["vo%d" % d], 2)
-                S.activation(T.tl[:, 1024 * d:1024 * d + NS], T.pgb[:, 0:4096].indirect(T.off[:, 64 * d:64 * d + NS // 16]), COPY).then_inc(sem["sg%d" % d], 1)
-        else:
-            if x[0] == flow[0]:
-                P.wait_ge(sem.qw8, 1)
-            for d in x:
-                product(d)
-                n, k = 2 * item[d], PW * src[d]
-                V.wait_ge(sem["pe%d" % n], 1)
-                V.tensor_copy(T.ysb[:, k:k + PW], T.ps[:, bank(n):bank(n) + 128]).then_inc(sem["ev%d" % n], 1)
-                n, k = n + 1, k + PW * N
-                S.wait_ge(sem["pe%d" % n], 1)
-                S.activation(T.ysb[:, k:k + PW], T.ps[:, bank(n):bank(n) + 128], COPY).then_inc(sem["ev%d" % n], 1)
-            store(S, x, 1)
+    S.wait_ge(sem.ldp, 16 * PG)
+    for d in GATHERS:
+        S.wait_ge(sem["vo%d" % d], 2)
+        S.activation(T.tl[:, 1024 * d:1024 * d + NS], T.pgb[:, 0:4096].indirect(T.off[:, 64 * d:64 * d + NS // 16]), COPY).then_inc(sem["sg%d" % d], 1)
+    for gr in OUTS:
+        for d in gr:
+            n, k = 2 * item[d] + 1, PW * (src[d] + N)
+            S.wait_ge(sem["pe%d" % n], 1)
+            S.activation(T.ysb[:, k:k + PW], T.ps[:, bank(n):bank(n) + 128], COPY).then_inc(sem["ev%d" % n], 1)
+        store(S, gr, 1)
 
     sent = 0
     front = [(owner(rank, k), k) for k in range(NB1)]
@@ -360,31 +362,30 @@ def rank_program(g, core, T, topo):
                             for i, d in enumerate(slots)], local_sem=sem.sent)
         return len(slots)
 
-    told = [False]
-    for d in served:
-        if d == OWN:
-            continue
-        if colof(d)[0] == 2 and not told[0]:
+    for d in [x for kind, x in steps if kind == "q" and x != OWN]:
+        if d == NB1:
             sent += choices(1, list(range(NB1)) + [MATE])
-            told[0] = True
+        if d == NR - 1:
+            sent += choices(2, list(range(NB1, NR)))
         sent += pages(d)
-    sent += choices(2, list(range(NB1, NR)))
 
     Y.wait_ge(sem.cfs0, 1)
     Y.dma_start(T.chs[0:2, rank:rank + 1], T.cf[0:1, 0:2]).then_inc(sem.chf, 16)
     for b in (1, 2):
         Y.wait_ge(sem["cfs%d" % b], 1)
         Y.dma_start(T.csrc[b], T.cf[0:8, 32 * b:32 * b + 32]).then_inc(sem["cd%d" % b], 16)
-    groups = [x for kind, x in PLAN if kind == "out"]
-    for i, gr in enumerate(groups):
-        if i == len(groups) - 2:
+        if b == 1:
+            Y.dma_start(T.qwb[:], T.qw[:]).then_inc(sem.ldq, 16)
+    for i, gr in enumerate(OUTS):
+        if i == 2:
             Y.wait_ge(sem.cl, N - 1)
             for d in range(NR + 1):
                 q, c = src[d], colof(d)[1] // 2
                 Y.dma_start(T.chs[0:2, q:q + 1], T.cland[q, c:c + 1, 0:2]).then_inc(sem.chf, 16)
+        if i == 4:
+            Y.wait_ge(sem.chf, 16 * N)
+            Y.dma_start(T.ch[:], T.chs[0:2, 0:8]).then_inc(sem.chd, 16)
         store(Y, gr, 0)
-    Y.wait_ge(sem.chf, 16 * N)
-    Y.dma_start(T.ch[:], T.chs[0:2, 0:8]).then_inc(sem.chd, 16)
     Y.wait_ge(sem.chd, 16)
     Y.wait_ge(sem.std, stores[0])
     g.wait_ge(sem.sent, sent)

from concourse.bass import DstId, RemoteDMATransfer
from concourse.mybir import dt, AluOpType, ActivationFunctionType

U8 = dt.uint8
N, PG, PW = 8, 8, 128
NR = 6
ROUNDS = [(2, 0, True), (1, 0, False), (1, 1, True), (2, 1, False), (3, 0, True), (3, 1, False)]
NB1 = 3
MATE, OWN = 6, 7
NS = 640
VPLAN = "c0 c1 o0 o1 n1 g0 o2 q0 g1 o7 q1 g2 q2 c2 o3 o4 n2 g3 o5 q3 g4 o6 q4 g5 q5 w0 g6 q6 g7 q7 e0 e1 e2 e3 e4"
GATHERS = [0, 1, 2, OWN, 3, 4, 5, MATE]
OUTS = [[0, 3], [1, 2], [OWN, MATE], [5], [4]]
LATE = 1

SCRATCH = {
    "gsb": ("sbuf", [128, 512], "bfloat16"),
    "smb": ("sbuf", [128, 512], "bfloat16"),
    "qwb": ("sbuf", [128, 1024], "bfloat16"),
    "pgb": ("sbuf", [128, 4096], "bfloat16"),
    "tl": ("sbuf", [128, 8192], "bfloat16"),
    "gt": ("sbuf", [128, 142], "float8_e4m3fn_x4"),
    "gtp": ("sbuf", [128, 142], "uint8"),
    "sc": ("sbuf", [128, 224], "float8_e4m3fn_x4"),
    "scp": ("sbuf", [128, 224], "uint8"),
    "wc": ("sbuf", [128, 256], "float8_e4m3fn_x4"),
    "wp": ("sbuf", [128, 256], "uint8"),
    "tc": ("sbuf", [128, 2048], "float8_e4m3fn_x4"),
    "tp": ("sbuf", [128, 2048], "uint8"),
    "rc": ("sbuf", [128, 2048], "float8_e4m3fn_x4"),
    "rp": ("sbuf", [128, 2048], "uint8"),
    "hc": ("sbuf", [128, 256 * NR], "float8_e4m3fn_x4"),
    "hp": ("sbuf", [128, 256 * NR], "uint8"),
    "hgc": ("sbuf", [128, 2], "float8_e4m3fn_x4"),
    "hgp": ("sbuf", [128, 2], "uint8"),
    "st": ("sbuf", [128, 96], "float32"),
    "pm": ("sbuf", [128, 24], "float32"),
    "lt": ("sbuf", [128, 192], "float32"),
    "zz": ("sbuf", [128, 64], "float32"),
    "ac": ("sbuf", [128, 192], "float32"),
    "ct": ("sbuf", [128, 96], "float32"),
    "cf": ("sbuf", [128, 96], "float32"),
    "iop": ("sbuf", [128, 2], "int32"),
    "ihi": ("sbuf", [128, 2], "int32"),
    "fhi": ("sbuf", [128, 2], "float32"),
    "io0": ("sbuf", [128, 32], "float32"),
    "io1": ("sbuf", [128, 32], "float32"),
    "off": ("sbuf", [128, 512], "uint16"),
    "ysb": ("sbuf", [128, 2048], "float32"),
    "chs": ("sbuf", [128, 8], "float32"),
    "csrc": ("dram", [3, 128, 2], "float32"),
    "cland": ("dram", [8, 128, 2], "float32"),
    "ps": ("psum", [128, 4096], "float32"),
}
SEMAPHORES = (["ldg", "lds", "ldq", "ldp", "ms", "qg", "qs", "qw8", "cst", "ga1", "ga2", "cl", "sent", "hgc", "hgp", "std", "chf", "chd"]
              + ["%s%d" % (n, b) for n in ("cps", "vc", "cfs", "cd") for b in range(3)]
              + ["%s%d" % (n, d) for n in ("vo", "vg", "sg", "vq", "arr") for d in range(8)]
              + ["%s%d" % (n, k) for n in ("hkc", "hkp") for k in range(NR)]
              + ["%s%d" % (n, d) for n in ("pe", "ev") for d in range(16)])


def bits(engines):
    m = 0
    for e in engines:
        m |= 1 << e
    return m


def layout(T, topo):
    cores = list(T.cores)
    chips = []
    for c in cores:
        if topo.chip(c) not in chips:
            chips.append(topo.chip(c))
    rows = [[r for r in range(N) if topo.chip(cores[r]) == ch] for ch in chips]
    place = {r: (x, y) for x in range(len(rows)) for y, r in enumerate(rows[x])}
    nx = len(rows)

    def asker(q, k):
        x, y = place[q]
        return rows[(x + ROUNDS[k][0]) % nx][y ^ ROUNDS[k][1]]

    def owner(r, k):
        x, y = place[r]
        return rows[(x - ROUNDS[k][0]) % nx][y ^ ROUNDS[k][1]]

    def mate(r):
        x, y = place[r]
        return rows[x][y ^ 1]

    def helper(r):
        c = cores[r]
        far = [d for d in cores if topo.chip(d) != topo.chip(c)]
        able = [h for h in topo.cores_of(c) if topo.die(h) != topo.die(c) and all(topo.may_write(h, d) for d in far)]
        return able[place[r][1]]

    return cores, asker, owner, mate, helper


def dest(topo, core):
    rid, pid, _ = topo.addr(core)
    return DstId(rid=rid, pnc=pid)


def write(g, topo, dst, out, in_, remote_sem, local_sem, engines):
    rid, pid, _ = topo.addr(dst)
    g.remote_dma(out, in_, remote_sem, local_sem, pid, rid, bits(engines))


def gslot(k):
    return k if k < NB1 else (NB1 if k == MATE else k + 1)


def gcols(k):
    return slice(128 + 2 * gslot(k), 130 + 2 * gslot(k))


def fan(g, T, topo, core, cores, owners, out, in_, semname):
    engines = topo.engines(core, cores[owners[0][0]])
    g.remote_dma_fused([RemoteDMATransfer(
        dst_ids=[dest(topo, cores[q]) for q, k in owners], dma_engine_mask=bits(engines), remote_sem=T.sem[semname],
        srcs=[in_], dsts=[out(k) for q, k in owners], alu_op=0)], local_sem=T.sem.sent)
    return len(engines)


def stay(topo, core, near, far):
    leave = topo.engines(core, far)
    return [e for e in topo.engines(core, near) if e not in leave]


def helper_program(g, core, T, topo, r, lay):
    cores, asker, owner, mate, helper = lay
    sent = 0
    back = [(owner(r, k), k) for k in range(NB1, NR)]
    half = len(stay(topo, cores[r], core, cores[back[0][0]])) // 2
    g.wait_ge(T.sem.hgc, half)
    sent += fan(g, T, topo, core, cores, back, lambda k: T.gt[:, gcols(k)].bitcast(U8), T.hgc[:, 0:2].bitcast(U8), "ga2")
    g.wait_ge(T.sem.hgp, half)
    sent += fan(g, T, topo, core, cores, back, lambda k: T.gtp[:, gcols(k)], T.hgp[:, 0:2], "ga2")
    for k in range(NR):
        if not ROUNDS[k][2]:
            continue
        a = cores[asker(r, k)]
        off = topo.engines(core, a)
        n = len(stay(topo, cores[r], core, a))
        s, d = slice(256 * k, 256 * k + 256), slice(256 * r, 256 * r + 256)
        g.wait_ge(T.sem["hkc%d" % k], n)
        write(g, topo, a, T.rc[:, d].bitcast(U8), T.hc[:, s].bitcast(U8), T.sem["arr%d" % r], T.sem.sent, off)
        g.wait_ge(T.sem["hkp%d" % k], n)
        write(g, topo, a, T.rp[:, d], T.hp[:, s], T.sem["arr%d" % r], T.sem.sent, off)
        sent += 2 * len(off)
    g.wait_ge(T.sem.sent, sent)


def rank_program(g, core, T, topo):
    lay = layout(T, topo)
    cores, asker, owner, mate, helper = lay
    rank = T.rank_of(core)
    if rank is None:
        for r in range(N):
            if helper(r) == core:
                helper_program(g, core, T, topo, r, lay)
        return
    V, S, P, Y, sem = g.vector, g.scalar, g.tensor, g.sync, T.sem
    A, COPY = AluOpType, ActivationFunctionType.Copy
    m, h = mate(rank), helper(rank)
    off = topo.engines(core, cores[asker(rank, 0)])
    loc = stay(topo, core, cores[m], cores[asker(rank, 0)])
    lh = len(loc) // 2
    who = [asker(rank, k) for k in range(NR)] + [m, rank]
    src = [owner(rank, k) for k in range(NR)] + [m, rank]
    steps = [(t[0], int(t[1])) for t in VPLAN.split()]
    flow = [d for gr in OUTS for d in gr]
    item = {d: i for i, d in enumerate(flow)}

    Y.dma_start(T.gsb[:, 0:256], T.gs[:, 0:256]).then_inc(sem.ldg, 16)
    S.dma_start(T.gsb[:, 256:512], T.gs[:, 256:512]).then_inc(sem.ldg, 16)
    Y.dma_start(T.smb[:], T.sm[:]).then_inc(sem.lds, 16)
    for p in range(PG):
        q = S if p % 2 == 0 or p >= PG - LATE else Y
        if p == PG - LATE:
            S.wait_ge(sem.vc0, 5)
        q.dma_start(T.pgb[:, 512 * p:512 * p + 512], T.pg[128 * p:128 * p + 128, :]).then_inc(sem.ldp, 16)

    V.memset(T.lt[:], 0.0).then_inc(sem.ms, 1)
    V.memset(T.zz[:], 0.0).then_inc(sem.ms, 1)
    g.iota(T.iop[:], [[0, 2]], 0, 1).then_inc(sem.cst, 1)
    g.iota(T.io0[:], [[16, 32]], 0, 1, allow_small_or_imprecise_dtypes=True).then_inc(sem.cst, 1)
    V.wait_ge(sem.cst, 2)
    V.tensor_scalar(T.ihi[:], T.iop[:], 112, None, A.bitwise_and).then_inc(sem.cst, 1)
    V.wait_ge(sem.cst, 3)
    V.tensor_copy(T.fhi[:], T.ihi[:]).then_inc(sem.cst, 1)
    V.wait_ge(sem.cst, 4)
    V.tensor_scalar(T.io1[:], T.io0[:], T.fhi[:, 0:1], None, A.subtract).then_inc(sem.cst, 1)
    V.wait_ge(sem.cst, 5)
    V.wait_ge(sem.ms, 2)
    V.wait_ge(sem.ldg, 32)
    V.quantize_mx(T.gt[:, 0:128], T.gtp[:, 0:128], T.gsb[:]).then_inc(sem.qg, 1)
    V.wait_ge(sem.lds, 16)
    for a in range(4):
        if a:
            V.wait_ge(sem.qs, a)
        V.quantize_mx(T.sc[:, 32 * a:32 * a + 128], T.scp[:, 32 * a:32 * a + 128], T.smb[:]).then_inc(sem.qs, 1)

    ends = [128, 128 + 2 * (NB1 + 1), 142]
    low = [0, 96, 96]
    head = [0, 32 - 2 * (NB1 + 1), 32 - 2 * (NR - NB1)]

    def colof(d):
        if d == OWN:
            return 0, 0
        if d == MATE or d < NB1:
            return 1, head[1] + 2 * gslot(d)
        return 2, head[2] + 2 * (d - NB1)

    def choice(b):
        c, e = 32 * b, 64 * b
        vc = sem["vc%d" % b]
        V.wait_ge(sem["cps%d" % b], 1)
        V.transpose(T.st[:, c:c + 32], T.ps[:, low[b]:low[b] + 32]).then_inc(vc, 1)
        V.wait_ge(vc, 1)
        V.tensor_tensor_scan(T.pm[:, 8 * b:8 * b + 8], T.st[:, c:c + 8], T.st[:, c:c + 8], T.st[:, c:c + 1], A.max, A.max).then_inc(vc, 1)
        V.wait_ge(vc, 2)
        V.tensor_scalar(T.lt[:, e + 24:e + 32], T.pm[:, 8 * b:8 * b + 8], T.pm[:, 8 * b + 7:8 * b + 8], 512.0, A.is_lt, A.mult).then_inc(vc, 1)
        V.wait_ge(vc, 3)
        V.tensor_tensor_scan(T.ac[:, e + 24:e + 64], T.lt[:, e + 24:e + 64], T.zz[:, 24:64], 0.0, A.add, A.add).then_inc(vc, 1)
        V.wait_ge(vc, 4)
        V.transpose(T.ct[:, c:c + 32], T.ac[:, e + 32:e + 64]).then_inc(vc, 1)
        V.wait_ge(vc, 5)

    def numbers(b):
        c = 32 * b
        V.tensor_scalar(T.cf[:, c:c + 32], T.ct[:, c:c + 32], 1.0 / 512, None, A.mult).then_inc(sem["cfs%d" % b], 1)

    def offsets(d):
        b, c = colof(d)
        for j in range(2):
            k = 64 * d + 32 * j
            V.tensor_scalar(T.off[:, k:k + 32], T.io1[:], T.ct[:, 32 * b + c + j:32 * b + c + j + 1], None, A.add).then_inc(sem["vo%d" % d], 1)

    arrived = [0, 2 * len(off) * NB1 + 2 * lh, 2 * len(off) * (NR - NB1)]

    def scores(b):
        if b:
            P.wait_ge(sem["vc%d" % (b - 1)], 1)
            P.wait_ge(sem["ga%d" % b], arrived[b])
        else:
            P.wait_ge(sem.qg, 1)
            P.wait_ge(sem.qs, 4)
        v = slice(ends[b] - 128, ends[b])
        P.matmul_mx(T.ps[:, 0:128], T.sc[:, 0:128], T.scp[:, 0:128], T.gt[:, v], T.gtp[:, v], True, True).then_inc(sem["cps%d" % b], 1)

    def bank(n):
        return 512 * (1 + n % 7)

    def product(d):
        if d == OWN:
            P.wait_ge(sem["vq%d" % OWN], 1)
            buf, pl, c0 = T.tc, T.tp, 256 * OWN
        else:
            P.wait_ge(sem["arr%d" % src[d]], 2 * (len(loc) if d == MATE else len(off)))
            buf, pl, c0 = T.rc, T.rp, 256 * src[d]
        for j in range(2):
            n = 2 * item[d] + j
            if n >= 7:
                P.wait_ge(sem["ev%d" % (n - 7)], 1)
            c, w = slice(c0 + 128 * j, c0 + 128 * j + 128), slice(128 * j, 128 * j + 128)
            P.matmul_mx(T.ps[:, bank(n):bank(n) + 128], T.wc[:, w], T.wp[:, w], buf[:, c], pl[:, c], True, True).then_inc(sem["pe%d" % n], 1)

    for b in range(3):
        scores(b)
    P.wait_ge(sem.qw8, 1)
    for d in flow:
        product(d)

    for kind, x in steps:
        if kind == "c":
            choice(x)
            if x == 0:
                numbers(0)
            if x == 1:
                V.wait_ge(sem.ldp, 16 * PG)
        elif kind == "w":
            V.wait_ge(sem.ldq, 16)
            V.quantize_mx(T.wc[:], T.wp[:], T.qwb[:]).then_inc(sem.qw8, 1)
        elif kind == "o":
            offsets(x)
        elif kind == "n":
            numbers(x)
        elif kind == "g":
            V.wait_ge(sem["vo%d" % x], 2)
            V.tensor_copy(T.tl[:, 1024 * x + NS:1024 * x + 1024],
                          T.pgb[:, 0:4096].indirect(T.off[:, 64 * x + NS // 16:64 * x + 64])).then_inc(sem["vg%d" % x], 1)
        elif kind == "q":
            V.wait_ge(sem["vg%d" % x], 1)
            V.wait_ge(sem["sg%d" % x], 1)
            V.quantize_mx(T.tc[:, 256 * x:256 * x + 256], T.tp[:, 256 * x:256 * x + 256], T.tl[:, 1024 * x:1024 * x + 1024]).then_inc(sem["vq%d" % x], 1)
        else:
            for d in OUTS[x]:
                n, k = 2 * item[d], PW * src[d]
                V.wait_ge(sem["pe%d" % n], 1)
                V.tensor_copy(T.ysb[:, k:k + PW], T.ps[:, bank(n):bank(n) + 128]).then_inc(sem["ev%d" % n], 1)

    stores = [0]

    def store(q, gr, j):
        qs = sorted(src[d] for d in gr)
        for d in gr:
            q.wait_ge(sem["ev%d" % (2 * item[d] + j)], 1)
        runs = [[qs[0]]]
        for x in qs[1:]:
            if x == runs[-1][-1] + 1:
                runs[-1].append(x)
            else:
                runs.append([x])
        for run in runs:
            a, b = PW * (j * N + run[0]), PW * (j * N + run[-1] + 1)
            q.dma_start(T.y[:, a:b], T.ysb[:, a:b]).then_inc(sem.std, 16)
            stores[0] += 16

    S.wait_ge(sem.ldp, 16 * PG)
    for d in GATHERS:
        S.wait_ge(sem["vo%d" % d], 2)
        S.activation(T.tl[:, 1024 * d:1024 * d + NS], T.pgb[:, 0:4096].indirect(T.off[:, 64 * d:64 * d + NS // 16]), COPY).then_inc(sem["sg%d" % d], 1)
    for gr in OUTS:
        for d in gr:
            n, k = 2 * item[d] + 1, PW * (src[d] + N)
            S.wait_ge(sem["pe%d" % n], 1)
            S.activation(T.ysb[:, k:k + PW], T.ps[:, bank(n):bank(n) + 128], COPY).then_inc(sem["ev%d" % n], 1)
        store(S, gr, 1)

    sent = 0
    front = [(owner(rank, k), k) for k in range(NB1)]
    g.wait_ge(sem.qg, 1)
    sent += fan(g, T, topo, core, cores, front, lambda k: T.gt[:, gcols(k)].bitcast(U8), T.gt[:, 0:2].bitcast(U8), "ga1")
    sent += fan(g, T, topo, core, cores, front, lambda k: T.gtp[:, gcols(k)], T.gtp[:, 0:2], "ga1")

    def near(outs, in_, sems):
        g.remote_dma_fused([RemoteDMATransfer(dst_ids=[dest(topo, c)], dma_engine_mask=bits(loc[lh * i:lh * i + lh]), remote_sem=sems[i],
                                              srcs=[in_], dsts=[outs[i]], alu_op=0) for i, c in enumerate((h, cores[m]))], local_sem=sem.sent)
        return 2 * lh

    sent += near([T.hgc[:, 0:2].bitcast(U8), T.gt[:, gcols(MATE)].bitcast(U8)], T.gt[:, 0:2].bitcast(U8), [sem.hgc, sem.ga1])
    sent += near([T.hgp[:, 0:2], T.gtp[:, gcols(MATE)]], T.gtp[:, 0:2], [sem.hgp, sem.ga1])

    def pages(d):
        s, t = slice(256 * d, 256 * d + 256), slice(256 * rank, 256 * rank + 256)
        g.wait_ge(sem["vq%d" % d], 1)
        if d < NR and ROUNDS[d][2]:
            write(g, topo, h, T.hc[:, s].bitcast(U8), T.tc[:, s].bitcast(U8), sem["hkc%d" % d], sem.sent, loc)
            write(g, topo, h, T.hp[:, s], T.tp[:, s], sem["hkp%d" % d], sem.sent, loc)
            return 2 * len(loc)
        e, a = (loc if d == MATE else off), cores[who[d]]
        write(g, topo, a, T.rc[:, t].bitcast(U8), T.tc[:, s].bitcast(U8), sem["arr%d" % rank], sem.sent, e)
        write(g, topo, a, T.rp[:, t], T.tp[:, s], sem["arr%d" % rank], sem.sent, e)
        return 2 * len(e)

    def choices(b, slots):
        g.wait_ge(sem["cd%d" % b], 16)
        g.remote_dma_fused([RemoteDMATransfer(dst_ids=[dest(topo, cores[who[d]])], dma_engine_mask=bits([loc[0] if d == MATE else off[i]]),
                                              remote_sem=sem.cl, srcs=[T.csrc[b]], dsts=[T.cland[rank]], alu_op=0)
                            for i, d in enumerate(slots)], local_sem=sem.sent)
        return len(slots)

    for d in [x for kind, x in steps if kind == "q" and x != OWN]:
        if d == NB1:
            sent += choices(1, list(range(NB1)) + [MATE])
        if d == NR - 1:
            sent += choices(2, list(range(NB1, NR)))
        sent += pages(d)

    Y.wait_ge(sem.cfs0, 1)
    Y.dma_start(T.chs[0:2, rank:rank + 1], T.cf[0:1, 0:2]).then_inc(sem.chf, 16)
    for b in (1, 2):
        Y.wait_ge(sem["cfs%d" % b], 1)
        Y.dma_start(T.csrc[b], T.cf[0:8, 32 * b:32 * b + 32]).then_inc(sem["cd%d" % b], 16)
        if b == 1:
            Y.dma_start(T.qwb[:], T.qw[:]).then_inc(sem.ldq, 16)
    for i, gr in enumerate(OUTS):
        if i == 2:
            Y.wait_ge(sem.cl, N - 1)
            for d in range(NR + 1):
                q, c = src[d], colof(d)[1] // 2
                Y.dma_start(T.chs[0:2, q:q + 1], T.cland[q, c:c + 1, 0:2]).then_inc(sem.chf, 16)
        if i == 4:
            Y.wait_ge(sem.chf, 16 * N)
            Y.dma_start(T.ch[:], T.chs[0:2, 0:8]).then_inc(sem.chd, 16)
        store(Y, gr, 0)
    Y.wait_ge(sem.chd, 16)
    Y.wait_ge(sem.std, stores[0])
    g.wait_ge(sem.sent, sent)
